import numpy as np
import ml_dtypes


def mxq(x, axis, fmt="e4m3"):
    dtype, down = {"e4m3": (ml_dtypes.float8_e4m3fn, 7), "e5m2": (ml_dtypes.float8_e5m2, 14)}[fmt]
    v = np.moveaxis(np.asarray(x, np.float32).astype(ml_dtypes.bfloat16).astype(np.float64), axis, -1)
    blocks = v.reshape(v.shape[:-1] + (-1, 32))
    amax = np.abs(blocks).max(-1, keepdims=True)
    byte = np.maximum(np.where(amax > 0, np.frexp(amax)[1] - 1 + 127, 0) - down, 1)
    scale = np.exp2(byte - 127.0)
    codes = (blocks / scale).astype(np.float32).astype(dtype).astype(np.float64)
    return np.moveaxis((codes * scale).reshape(v.shape), -1, axis)


WIDE = False


def mx_kscale(k):
    if not WIDE:
        return np.ones(k)
    levels = np.array([10, -10, 5, -5, 0])
    if k % 512:
        return np.exp2(np.random.permutation(np.resize(levels, k // 32))).repeat(32)
    a = np.empty((k // 512, 16))
    for p in range(k // 512):
        a[p, :8] = np.random.permutation(np.resize(levels, 8))
        for g in range(8):
            far = levels[np.abs(levels - a[p, g]) >= 10]
            a[p, g + 8] = far[np.random.randint(len(far))]
    return np.exp2(a.ravel()).repeat(32)


def f64(x):
    return np.asarray(x).astype(np.float64)


def striped(idx):
    return np.tile(idx.reshape(-1, 16).T, (8, 1)).astype(np.uint16)


def unstriped(offs):
    return offs[:16].T.reshape(-1).astype(np.int64)


def striped8(idx):
    return np.concatenate([x.reshape(-1, 16).T for x in idx]).astype(np.uint16)


def runs(offs, k):
    lists = np.stack([offs[16 * r : 16 * r + 16].T.reshape(-1) for r in range(8)]).astype(np.int64)
    return lists[np.arange(k) % 512 // 64]


def pack_weight(w):
    k, n = w.shape
    w = f64(np.asarray(w, np.float32).astype(ml_dtypes.bfloat16)).reshape(k // 32, 32, n)
    amax = np.abs(w).max(1)
    byte = np.clip(np.where(amax > 0, np.frexp(amax)[1] - 1 + 127 - 7, 1), 1, 254)
    scaled = (w * np.exp2(127.0 - byte)[:, None, :]).reshape(k, n).astype(np.float32)
    words = np.ascontiguousarray(scaled.reshape(k // 512, 128, 4, n).transpose(0, 1, 3, 2)).astype(ml_dtypes.float8_e4m3fn).view(np.uint8)
    return words, np.ascontiguousarray(byte.astype(np.uint8).reshape(k // 512, 16, n))


def unpack_weight(words, scales):
    g, p, n, _ = words.shape
    vals = np.ascontiguousarray(words).view(ml_dtypes.float8_e4m3fn).astype(np.float64) * np.repeat(np.exp2(scales.astype(np.float64) - 127.0), 8, axis=1)[..., None]
    return vals.transpose(0, 1, 3, 2).reshape(g * 512, n)


def sigmoid(v):
    return 1.0 / (1.0 + np.exp(-np.maximum(v, -700.0)))


K, T, S, H, G = 512, 1024, 512, 512, 2048


def setup_inputs():
    n = np.random.standard_normal
    s = mx_kscale(K)[:, None]
    packed_xT = pack_weight(n((K, T)) * s)
    packed_dT = pack_weight(n((K, G)) / s)
    return {
        "x_words": packed_xT[0],
        "x_scales": packed_xT[1],
        "w1": (n((K, H)) / np.sqrt(2 * K) / s).astype(np.float32),
        "w2": (n((K, H)) / np.sqrt(2 * K) / s).astype(np.float32),
        "sl": np.random.uniform(1.0, 2.0, (H, 1)).astype(np.float32),
        "th": (0.5 * n((H, 1))).astype(np.float32),
        "gs": (np.random.uniform(0.5, 1.5, (K, 1)) * s).astype(np.float32),
        "d_words": packed_dT[0],
        "d_scales": packed_dT[1],
        "offs": striped(np.random.permutation(T)[:S]),
        "hz": striped8(np.random.randint(0, T, (8, S))),
        "n1": striped8(np.stack([np.random.permutation(S) for _ in range(8)])),
        "n2": striped8(np.stack([np.random.permutation(S) for _ in range(8)])),
        "ka": striped8(np.random.randint(0, G, (8, H))),
        "kb": striped8(np.random.randint(0, G, (8, H))),
        "n3": striped8(np.stack([np.random.permutation(S) for _ in range(8)])),
        "n4": striped8(np.stack([np.random.permutation(S) for _ in range(8)])),
    }


def reference(x_words, x_scales, w1, w2, sl, th, gs, d_words, d_scales, offs, hz, n1, n2, ka, kb, n3, n4):
    d_ka = unpack_weight(d_words, d_scales)[np.arange(K)[:, None], runs(ka, K)]
    xq = unpack_weight(x_words, x_scales)[:, unstriped(offs)]
    x_hz = unpack_weight(x_words, x_scales)[np.arange(K)[:, None], runs(hz, K)]
    y = mxq(f64(w1), 0, "e4m3").T @ xq + mxq(f64(w2), 0, "e4m3").T @ x_hz
    ds = np.zeros((H, S))
    ds[np.arange(H)[:, None], runs(n1, H)] = y
    sg = sigmoid(f64(sl) * (y[np.arange(H)[:, None], runs(n2, H)] - f64(th)))
    z = f64(gs) * (ds * sg)
    zq = mxq(z, 0, "e4m3")
    d_kb = unpack_weight(d_words, d_scales)[np.arange(K)[:, None], runs(kb, K)]
    h2 = 0.0625 * (d_ka.T @ zq + d_kb.T @ zq)
    ds2 = np.zeros((H, S))
    ds2[np.arange(H)[:, None], runs(n3, H)] = h2
    st = np.maximum(h2, ds2)
    ds3 = np.zeros((H, S))
    ds3[np.arange(H)[:, None], runs(n4, H)] = st
    return st - ds3

@@ -1,0 +1,248 @@
+from contextlib import ExitStack
+
+import concourse.mybir as mybir
+
+F32 = mybir.dt.float32
+BF16 = mybir.dt.bfloat16
+I32 = mybir.dt.int32
+U32 = mybir.dt.uint32
+U16 = mybir.dt.uint16
+U8 = mybir.dt.uint8
+FP8X4 = mybir.dt.float8_e4m3fn_x4
+ALU = mybir.AluOpType
+ACT = mybir.ActivationFunctionType
+
+P = 128
+PACK = 4
+K, T, S, H, G = 512, 1024, 512, 512, 2048
+TILES = H // P
+RUN = 8
+HEAD = 128
+WIDE = 2 * S
+
+FLOPS = 2 * 2 * K * H * S + 2 * 2 * K * H * S
+
+
+def tile_picked_dthzaesndsndtwin_none_p_kernel(
+    tc, x_words, x_scales, w1, w2, sl, th, gs, d_words, d_scales, offs, hz, n1, n2, ka, kb, n3, n4, out
+):
+    nc = tc.nc
+    with ExitStack() as ctx:
+        lists = ctx.enter_context(tc.tile_pool(name="lists", bufs=1))
+        keep = ctx.enter_context(tc.tile_pool(name="keep", bufs=1))
+        psum = ctx.enter_context(tc.psum_pool(name="psum", bufs=1))
+
+        def tile(name, shape, dtype):
+            return keep.tile(shape, dtype, name=name, align_bytes=64)
+
+        def load_list(name, src):
+            dst = lists.tile([P, S // 16], U16, name=name)
+            nc.sync.dma_start(dst[:], src)
+            return dst
+
+        def load_scales(name, scales, width):
+            dst = tile(name, [P, width], U8)
+            rows = scales[0].bitcast(I32).unsqueeze(1).to_broadcast([16, 8, width // 4])
+            nc.sync.dma_start(dst[:].bitcast(I32), rows)
+            return dst
+
+        def load_words(name, words, width):
+            dst = tile(name, [P, width], U32)
+            nc.sync.dma_start(dst[:].bitcast(I32), words[0].rearrange("p n t -> p (n t)").bitcast(I32))
+            return dst
+
+        def load_weight(name, w):
+            dst = tile(name, [P, PACK, H], F32)
+            nc.scalar.dma_start(dst[:], w.rearrange("(p j) c -> p j c", j=PACK))
+            return dst
+
+        def load_column(name, v):
+            dst = tile(name, [P, TILES], F32)
+            nc.gpsimd.dma_start(dst[:], v.rearrange("(p t) o -> p (t o)", t=TILES))
+            return dst
+
+        def cols(lst, a, b):
+            return lst[:, a // 16 : b // 16]
+
+        w1_raw = load_weight("w1_raw", w1)
+        w2_raw = load_weight("w2_raw", w2)
+        offs_l = load_list("offs_l", offs)
+        xs_win = load_scales("xs_win", x_scales, T)
+        hz_l = load_list("hz_l", hz)
+        ka_l = load_list("ka_l", ka)
+        ds_win = load_scales("ds_win", d_scales, G)
+        kb_l = load_list("kb_l", kb)
+        xw_win = load_words("xw_win", x_words, T)
+        sl_c = load_column("sl_c", sl)
+        th_c = load_column("th_c", th)
+        gs_c = load_column("gs_c", gs)
+
+        s_pick = tile("s_pick", [P, 4 * S], U8)
+        nc.vector.tensor_copy(s_pick[:, 0:S], xs_win[:].indirect(offs_l[:]))
+        nc.vector.tensor_copy(s_pick[:, S : 2 * S], xs_win[:].indirect(hz_l[:]))
+        nc.vector.tensor_copy(s_pick[:, 2 * S : 3 * S], ds_win[:].indirect(ka_l[:]))
+        nc.vector.tensor_copy(s_pick[:, 3 * S : 4 * S], ds_win[:].indirect(kb_l[:]))
+        xs_plane = tile("xs_plane", [P, 4 * S], U8)
+        nc.vector.memset(xs_plane[:].bitcast(I32), 0)
+        for r in range(4):
+            nc.sync.dma_start(xs_plane[r:P:32, :].bitcast(I32), s_pick[8 * r : P : 32, :].bitcast(I32))
+
+        dw_win = load_words("dw_win", d_words, G)
+        n1_l = load_list("n1_l", n1)
+        n2_l = load_list("n2_l", n2)
+        n3_l = load_list("n3_l", n3)
+        n4_l = load_list("n4_l", n4)
+
+        def interleave_weight(name, raw):
+            grouped = tile(name, [P, TILES, P, PACK], BF16)
+            nc.scalar.copy(
+                grouped[:].rearrange("p t m j -> p m t j"),
+                raw[:].rearrange("p j (m t) -> p m t j", t=TILES),
+            )
+            return grouped
+
+        def quantize(name, grouped, width):
+            codes = tile(name + "_codes", [P, width], U32)
+            plane = tile(name + "_plane", [P, width], U8)
+            nc.vector.quantize_mx(out=codes[:].bitcast(FP8X4), scales=plane[:], in_=grouped)
+            return codes, plane
+
+        w1_g = interleave_weight("w1_g", w1_raw)
+        w2_g = interleave_weight("w2_g", w2_raw)
+        w1_codes, w1_plane = quantize("w1", w1_g[:].rearrange("p t m j -> p (t m j)"), H)
+
+        x_offs = tile("x_offs", [P, S], U32)
+        nc.vector.tensor_copy(x_offs[:], xw_win[:].indirect(offs_l[:]))
+        x_hz = tile("x_hz", [P, S], U32)
+        nc.vector.tensor_copy(x_hz[:], xw_win[:].indirect(hz_l[:]))
+        w2_codes, w2_plane = quantize("w2", w2_g[:].rearrange("p t m j -> p (t m j)"), H)
+
+        bias = tile("bias", [P, TILES], F32)
+        sl_th = tile("sl_th", [P, TILES], F32)
+        nc.gpsimd.tensor_tensor(sl_th[:], sl_c[:], th_c[:], ALU.mult)
+        nc.gpsimd.tensor_scalar(bias[:], sl_th[:], -1.0, 0.0, ALU.mult, ALU.add)
+
+        dw_pick = tile("dw_pick", [P, 2 * H], U32)
+        nc.vector.tensor_copy(dw_pick[:, 0:H], dw_win[:].indirect(ka_l[:]))
+        nc.vector.tensor_copy(dw_pick[:, H : 2 * H], dw_win[:].indirect(kb_l[:]))
+
+        ds_plane = tile("ds_plane", [P, 2 * H], U8)
+        nc.vector.tensor_copy(
+            ds_plane[:].bitcast(I32).rearrange("p (t a w) -> p t a w", t=TILES, w=RUN // 4),
+            xs_plane[:, 2 * S : 4 * S].bitcast(I32).rearrange("p (a t w) -> p t a w", t=TILES, w=RUN // 4),
+        )
+
+        dw_dealt = []
+        for t in range(TILES):
+            dealt = tile("dw_dealt%d" % t, [P, 2 * P], U32)
+            nc.sync.dma_start(
+                dealt[:].bitcast(I32).rearrange("p (a w) -> p a w", w=RUN),
+                dw_pick[:].bitcast(I32).rearrange("p (a t w) -> p t a w", t=TILES, w=RUN)[:, t],
+            )
+            dw_dealt.append(dealt)
+
+        y, sg = [], []
+        for t in range(TILES):
+            bank = psum.tile([P, S], F32, name="bank%d" % t)
+            m = slice(t * P, (t + 1) * P)
+            nc.tensor.matmul_mx(
+                out=bank[:], lhsT=w1_codes[:, m].bitcast(FP8X4), lhsT_scale=w1_plane[:, m],
+                rhs=x_offs[:].bitcast(FP8X4), rhs_scale=xs_plane[:, 0:S], start=True, stop=False,
+            )
+            nc.tensor.matmul_mx(
+                out=bank[:], lhsT=w2_codes[:, m].bitcast(FP8X4), lhsT_scale=w2_plane[:, m],
+                rhs=x_hz[:].bitcast(FP8X4), rhs_scale=xs_plane[:, S : 2 * S], start=False, stop=True,
+            )
+            y_t = tile("y%d" % t, [P, S], F32)
+            nc.scalar.copy(y_t[:], bank[:])
+            y.append(y_t)
+        for t in range(TILES):
+            sg_t = tile("sg%d" % t, [P, S], F32)
+            for a in range(0, S, S // 2):
+                nc.scalar.activation(
+                    out=sg_t[:, a : a + S // 2], in_=y[t][:].indirect(cols(n2_l, a, a + S // 2)),
+                    func=ACT.Sigmoid, scale=sl_c[:, t : t + 1], bias=bias[:, t : t + 1],
+                )
+            sg.append(sg_t)
+
+        z_rows = tile("z_rows", [P, TILES, S], BF16)
+        ds = []
+
+        def scatter(name, lst, src):
+            win = tile(name, [P, WIDE], F32)
+            nc.vector.tensor_copy(win[:].indirect(lst[:]), src[:])
+            return win
+
+        def make_z(t, a, b):
+            nc.vector.scalar_tensor_tensor(
+                z_rows[:, t, a:b], ds[t][:, a:b], gs_c[:, t : t + 1], sg[t][:, a:b], ALU.mult, ALU.mult
+            )
+
+        for t in range(TILES):
+            ds.append(scatter("ds_%d" % t, n1_l, y[t]))
+            if 0 < t < TILES - 1:
+                make_z(t - 1, 0, S)
+        make_z(TILES - 2, 0, S)
+        make_z(TILES - 1, 0, HEAD)
+        make_z(TILES - 1, HEAD, S)
+
+        pieces = [(0, HEAD), (HEAD, 2 * HEAD), (2 * HEAD, S)]
+        z_q = []
+        for i, (a, b) in enumerate(pieces):
+            grouped = tile("z_g%d" % i, [P, b - a, PACK], BF16)
+            src = z_rows[:, :, a:b].rearrange("p t c -> p c t")
+            if i == 0:
+                nc.vector.tensor_copy(grouped[:], src)
+            else:
+                nc.scalar.copy(grouped[:], src)
+            z_q.append(grouped)
+
+        h2 = [tile("h2_%d" % t, [P, S], F32) for t in range(TILES)]
+        ds2 = [tile("ds2_%d" % t, [P, WIDE], F32) for t in range(TILES)]
+
+        def second_product(acc, t, codes, plane):
+            for half in range(2):
+                m = slice(half * P, (half + 1) * P)
+                sm = slice(t * 2 * P + half * P, t * 2 * P + (half + 1) * P)
+                nc.tensor.matmul_mx(
+                    out=acc, lhsT=dw_dealt[t][:, m].bitcast(FP8X4), lhsT_scale=ds_plane[:, sm],
+                    rhs=codes[:].bitcast(FP8X4), rhs_scale=plane[:], start=(half == 0), stop=(half == 1),
+                )
+
+        codes, plane = quantize("z0", z_q[0][:].rearrange("p c t -> p (c t)"), HEAD)
+        for t in range(TILES):
+            bank = psum.tile([P, S], F32, name="bank%d" % t)
+            second_product(bank[:, 0:HEAD], t, codes, plane)
+            nc.scalar.activation(out=h2[t][:, 0:HEAD], in_=bank[:, 0:HEAD], func=ACT.Copy, scale=0.0625)
+        rest = [quantize("z%d" % i, z_q[i][:].rearrange("p c t -> p (c t)"), b - a) for i, (a, b) in enumerate(pieces) if i]
+        for t in range(TILES):
+            nc.vector.tensor_copy(ds2[t][:].indirect(cols(n3_l, 0, HEAD)), h2[t][:, 0:HEAD])
+        for t in range(TILES):
+            bank = psum.tile([P, S], F32, name="bank%d" % (TILES + t))
+            for (a, b), (codes, plane) in zip(pieces[1:], rest):
+                second_product(bank[:, a:b], t, codes, plane)
+            nc.scalar.activation(out=h2[t][:, HEAD:S], in_=bank[:, HEAD:S], func=ACT.Copy, scale=0.0625)
+
+        st = [tile("st_%d" % t, [P, S], F32) for t in range(TILES)]
+        ds3 = []
+        out_rows = out.rearrange("(a t w) c -> t a w c", t=TILES, w=RUN)
+
+        def larger(t):
+            nc.vector.tensor_tensor(st[t][:], h2[t][:], ds2[t][:, 0:S], ALU.max)
+
+        def finish(t):
+            res = tile("res_%d" % t, [P, S], F32)
+            nc.vector.tensor_tensor(res[:], st[t][:], ds3[t][:, 0:S], ALU.subtract)
+            nc.sync.dma_start(out_rows[t], res[:])
+
+        for t in range(TILES):
+            nc.vector.tensor_copy(ds2[t][:].indirect(cols(n3_l, HEAD, S)), h2[t][:, HEAD:S])
+            if t > 0:
+                larger(t - 1)
+        for t in range(TILES):
+            ds3.append(scatter("ds3_%d" % t, n4_l, st[t]))
+            if t == 0:
+                larger(TILES - 1)
+            else:
+                finish(t - 1)
+        finish(TILES - 1)

@@ -1,6 +1,7 @@
 from contextlib import ExitStack
 
 import concourse.mybir as mybir
+from concourse.masks import make_identity
 
 F32 = mybir.dt.float32
 BF16 = mybir.dt.bfloat16
@@ -32,8 +33,8 @@ def tile_picked_dthzaesndsndtwin_none_p_kernel(
         keep = ctx.enter_context(tc.tile_pool(name="keep", bufs=1))
         psum = ctx.enter_context(tc.psum_pool(name="psum", bufs=1))
 
-        def tile(name, shape, dtype):
-            return keep.tile(shape, dtype, name=name, align_bytes=64)
+        def tile(name, shape, dtype, tag=""):
+            return keep.tile(shape, dtype, name=name, tag=tag or name, align_bytes=64)
 
         def load_list(name, src):
             dst = lists.tile([P, S // 16], U16, name=name)
@@ -46,14 +47,14 @@ def tile_picked_dthzaesndsndtwin_none_p_kernel(
             nc.sync.dma_start(dst[:].bitcast(I32), rows)
             return dst
 
-        def load_words(name, words, width):
-            dst = tile(name, [P, width], U32)
+        def load_words(name, words, width, tag=""):
+            dst = tile(name, [P, width], U32, tag)
             nc.sync.dma_start(dst[:].bitcast(I32), words[0].rearrange("p n t -> p (n t)").bitcast(I32))
             return dst
 
         def load_weight(name, w):
             dst = tile(name, [P, PACK, H], F32)
-            nc.scalar.dma_start(dst[:], w.rearrange("(p j) c -> p j c", j=PACK))
+            nc.sync.dma_start(dst[:], w.rearrange("(p j) c -> p j c", j=PACK))
             return dst
 
         def load_column(name, v):
@@ -64,14 +65,14 @@ def tile_picked_dthzaesndsndtwin_none_p_kernel(
         def cols(lst, a, b):
             return lst[:, a // 16 : b // 16]
 
-        w1_raw = load_weight("w1_raw", w1)
-        w2_raw = load_weight("w2_raw", w2)
         offs_l = load_list("offs_l", offs)
         xs_win = load_scales("xs_win", x_scales, T)
         hz_l = load_list("hz_l", hz)
         ka_l = load_list("ka_l", ka)
         ds_win = load_scales("ds_win", d_scales, G)
         kb_l = load_list("kb_l", kb)
+        w1_raw = load_weight("w1_raw", w1)
+        w2_raw = load_weight("w2_raw", w2)
         xw_win = load_words("xw_win", x_words, T)
         sl_c = load_column("sl_c", sl)
         th_c = load_column("th_c", th)
@@ -87,11 +88,14 @@ def tile_picked_dthzaesndsndtwin_none_p_kernel(
         for r in range(4):
             nc.sync.dma_start(xs_plane[r:P:32, :].bitcast(I32), s_pick[8 * r : P : 32, :].bitcast(I32))
 
-        dw_win = load_words("dw_win", d_words, G)
+        dw_win = load_words("dw_win", d_words, G, "ds_win")
         n1_l = load_list("n1_l", n1)
         n2_l = load_list("n2_l", n2)
         n3_l = load_list("n3_l", n3)
         n4_l = load_list("n4_l", n4)
+
+        ident = tile("ident", [P, P], F32)
+        make_identity(nc, ident[:])
 
         def interleave_weight(name, raw):
             grouped = tile(name, [P, TILES, P, PACK], BF16)
@@ -223,26 +227,55 @@ def tile_picked_dthzaesndsndtwin_none_p_kernel(
                 second_product(bank[:, a:b], t, codes, plane)
             nc.scalar.activation(out=h2[t][:, HEAD:S], in_=bank[:, HEAD:S], func=ACT.Copy, scale=0.0625)
 
-        st = [tile("st_%d" % t, [P, S], F32) for t in range(TILES)]
-        ds3 = []
+        def open_bank(number):
+            return psum.tile([P, S], F32, name="bank%d" % number)
+
+        def add_turned(bank, term, first=False, last=False):
+            for b in range(0, S, P):
+                nc.tensor.matmul(
+                    bank[:, b : b + P], term[:, b : b + P], ident[:],
+                    start=(first and b == 0), stop=(last and b == S - P), is_transpose=True,
+                )
+
+        def leave(name, src, func, scale):
+            dst = tile(name, [P, S], F32)
+            nc.scalar.activation(out=dst[:], in_=src[:], func=func, scale=scale)
+            return dst
+
+        h2_turned, diff_bank, st_bank = [], [], []
+        for t in range(TILES):
+            h2_neg = leave("h2_neg%d" % t, h2[t], ACT.Copy, -1.0)
+            bank = open_bank(t)
+            add_turned(bank, h2[t], first=True, last=True)
+            h2_turned.append(leave("h2_turned%d" % t, bank, ACT.Copy, 1.0))
+            diff_bank.append(open_bank(TILES + t))
+            add_turned(diff_bank[t], h2_neg, first=True)
+            st_bank.append(open_bank(t))
+            add_turned(st_bank[t], h2_turned[t], first=True)
+
         out_rows = out.rearrange("(a t w) c -> t a w c", t=TILES, w=RUN)
-
-        def larger(t):
-            nc.vector.tensor_tensor(st[t][:], h2[t][:], ds2[t][:, 0:S], ALU.max)
-
-        def finish(t):
-            res = tile("res_%d" % t, [P, S], F32)
-            nc.vector.tensor_tensor(res[:], st[t][:], ds3[t][:, 0:S], ALU.subtract)
-            nc.sync.dma_start(out_rows[t], res[:])
-
+        st, out_bank = [], []
         for t in range(TILES):
             nc.vector.tensor_copy(ds2[t][:].indirect(cols(n3_l, HEAD, S)), h2[t][:, HEAD:S])
-            if t > 0:
-                larger(t - 1)
+            add_turned(diff_bank[t], ds2[t], last=True)
+            gain = leave("gain%d" % t, diff_bank[t], ACT.Relu, 1.0)
+            add_turned(st_bank[t], gain, last=True)
+            st.append(leave("st%d" % t, st_bank[t], ACT.Copy, 1.0))
+            if t < TILES - 1:
+                out_bank.append(open_bank(t))
+                add_turned(out_bank[t], h2_turned[t], first=True)
+                add_turned(out_bank[t], gain)
         for t in range(TILES):
-            ds3.append(scatter("ds3_%d" % t, n4_l, st[t]))
-            if t == 0:
-                larger(TILES - 1)
+            ds3 = scatter("ds3_%d" % t, n4_l, st[t])
+            if t < TILES - 1:
+                bank = open_bank(TILES + t)
+                add_turned(bank, ds3, first=True, last=True)
+                add_turned(out_bank[t], leave("ds3_neg%d" % t, bank, ACT.Copy, -1.0), last=True)
+                res = leave("res%d" % t, out_bank[t], ACT.Copy, 1.0)
+                nc.sync.dma_start(out_rows[t], res[:])
             else:
-                finish(t - 1)
-        finish(TILES - 1)
+                res = tile("res%d" % t, [P, S], F32)
+                for a, queue in ((0, nc.sync), (S // 2, nc.scalar)):
+                    half = slice(a, a + S // 2)
+                    nc.vector.tensor_tensor(res[:, half], st[t][:, half], ds3[:, half], ALU.subtract)
+                    queue.dma_start(out_rows[t][:, :, half], res[:, half])

@@ -18,7 +18,7 @@ PACK = 4
 K, T, S, H, G = 512, 1024, 512, 512, 2048
 TILES = H // P
 RUN = 8
-HEAD = 128
+HEAD = 256
 WIDE = 2 * S
 
 FLOPS = 2 * 2 * K * H * S + 2 * 2 * K * H * S
@@ -43,8 +43,8 @@ def tile_picked_dthzaesndsndtwin_none_p_kernel(
 
         def load_scales(name, scales, width):
             dst = tile(name, [P, width], U8)
-            rows = scales[0].bitcast(I32).unsqueeze(1).to_broadcast([16, 8, width // 4])
-            nc.sync.dma_start(dst[:].bitcast(I32), rows)
+            nc.gpsimd.memset(dst[:].bitcast(I32), 0)
+            nc.sync.dma_start(dst[0:P:8, :].bitcast(I32), scales[0].bitcast(I32))
             return dst
 
         def load_words(name, words, width, tag=""):
@@ -57,9 +57,9 @@ def tile_picked_dthzaesndsndtwin_none_p_kernel(
             nc.sync.dma_start(dst[:], w.rearrange("(p j) c -> p j c", j=PACK))
             return dst
 
-        def load_column(name, v):
-            dst = tile(name, [P, TILES], F32)
-            nc.gpsimd.dma_start(dst[:], v.rearrange("(p t) o -> p (t o)", t=TILES))
+        def load_column(name, v, tag):
+            dst = tile(name, [P, TILES], F32, tag)
+            nc.sync.dma_start(dst[:], v.rearrange("(p t) o -> p (t o)", t=TILES))
             return dst
 
         def cols(lst, a, b):
@@ -74,9 +74,11 @@ def tile_picked_dthzaesndsndtwin_none_p_kernel(
         w1_raw = load_weight("w1_raw", w1)
         w2_raw = load_weight("w2_raw", w2)
         xw_win = load_words("xw_win", x_words, T)
-        sl_c = load_column("sl_c", sl)
-        th_c = load_column("th_c", th)
-        gs_c = load_column("gs_c", gs)
+        n1_l = load_list("n1_l", n1)
+        n2_l = load_list("n2_l", n2)
+        n3_l = load_list("n3_l", n3)
+        n4_l = load_list("n4_l", n4)
+        dw_win = load_words("dw_win", d_words, G)
 
         s_pick = tile("s_pick", [P, 4 * S], U8)
         nc.vector.tensor_copy(s_pick[:, 0:S], xs_win[:].indirect(offs_l[:]))
@@ -88,43 +90,36 @@ def tile_picked_dthzaesndsndtwin_none_p_kernel(
         for r in range(4):
             nc.sync.dma_start(xs_plane[r:P:32, :].bitcast(I32), s_pick[8 * r : P : 32, :].bitcast(I32))
 
-        dw_win = load_words("dw_win", d_words, G, "ds_win")
-        n1_l = load_list("n1_l", n1)
-        n2_l = load_list("n2_l", n2)
-        n3_l = load_list("n3_l", n3)
-        n4_l = load_list("n4_l", n4)
+        sl_c = load_column("sl_c", sl, "xs_win")
+        th_c = load_column("th_c", th, "ds_win")
+        gs_c = load_column("gs_c", gs, "s_pick")
 
         ident = tile("ident", [P, P], F32)
         make_identity(nc, ident[:])
 
-        def interleave_weight(name, raw):
-            grouped = tile(name, [P, TILES, P, PACK], BF16)
-            nc.scalar.copy(
-                grouped[:].rearrange("p t m j -> p m t j"),
-                raw[:].rearrange("p j (m t) -> p m t j", t=TILES),
-            )
-            return grouped
-
-        def quantize(name, grouped, width):
-            codes = tile(name + "_codes", [P, width], U32)
+        def quantize(name, grouped, width, tag=""):
+            codes = tile(name + "_codes", [P, width], U32, tag)
             plane = tile(name + "_plane", [P, width], U8)
             nc.vector.quantize_mx(out=codes[:].bitcast(FP8X4), scales=plane[:], in_=grouped)
             return codes, plane
 
-        w1_g = interleave_weight("w1_g", w1_raw)
-        w2_g = interleave_weight("w2_g", w2_raw)
-        w1_codes, w1_plane = quantize("w1", w1_g[:].rearrange("p t m j -> p (t m j)"), H)
+        def quantize_weight_half(name, raw, half):
+            grouped = tile(name, [P, 2, P, PACK], BF16)
+            nc.scalar.copy(
+                grouped[:].rearrange("p t m j -> p m t j"),
+                raw[:].rearrange("p j (m t) -> p m t j", t=TILES)[:, :, 2 * half : 2 * half + 2, :],
+            )
+            return quantize(name, grouped[:].rearrange("p t m j -> p (t m j)"), 2 * P)
 
+        w1_q = [quantize_weight_half("w1_%d" % half, w1_raw, half) for half in range(2)]
         x_offs = tile("x_offs", [P, S], U32)
         nc.vector.tensor_copy(x_offs[:], xw_win[:].indirect(offs_l[:]))
         x_hz = tile("x_hz", [P, S], U32)
         nc.vector.tensor_copy(x_hz[:], xw_win[:].indirect(hz_l[:]))
-        w2_codes, w2_plane = quantize("w2", w2_g[:].rearrange("p t m j -> p (t m j)"), H)
+        w2_q = [quantize_weight_half("w2_%d" % half, w2_raw, half) for half in range(2)]
 
         bias = tile("bias", [P, TILES], F32)
-        sl_th = tile("sl_th", [P, TILES], F32)
-        nc.gpsimd.tensor_tensor(sl_th[:], sl_c[:], th_c[:], ALU.mult)
-        nc.gpsimd.tensor_scalar(bias[:], sl_th[:], -1.0, 0.0, ALU.mult, ALU.add)
+        nc.vector.scalar_tensor_tensor(bias[:], sl_c[:], -1.0, th_c[:], ALU.mult, ALU.mult)
 
         dw_pick = tile("dw_pick", [P, 2 * H], U32)
         nc.vector.tensor_copy(dw_pick[:, 0:H], dw_win[:].indirect(ka_l[:]))
@@ -148,7 +143,9 @@ def tile_picked_dthzaesndsndtwin_none_p_kernel(
         y, sg = [], []
         for t in range(TILES):
             bank = psum.tile([P, S], F32, name="bank%d" % t)
-            m = slice(t * P, (t + 1) * P)
+            m = slice(t % 2 * P, (t % 2 + 1) * P)
+            w1_codes, w1_plane = w1_q[t // 2]
+            w2_codes, w2_plane = w2_q[t // 2]
             nc.tensor.matmul_mx(
                 out=bank[:], lhsT=w1_codes[:, m].bitcast(FP8X4), lhsT_scale=w1_plane[:, m],
                 rhs=x_offs[:].bitcast(FP8X4), rhs_scale=xs_plane[:, 0:S], start=True, stop=False,
@@ -169,63 +166,48 @@ def tile_picked_dthzaesndsndtwin_none_p_kernel(
                 )
             sg.append(sg_t)
 
-        z_rows = tile("z_rows", [P, TILES, S], BF16)
-        ds = []
-
         def scatter(name, lst, src):
             win = tile(name, [P, WIDE], F32)
             nc.vector.tensor_copy(win[:].indirect(lst[:]), src[:])
             return win
 
-        def make_z(t, a, b):
-            nc.vector.scalar_tensor_tensor(
-                z_rows[:, t, a:b], ds[t][:, a:b], gs_c[:, t : t + 1], sg[t][:, a:b], ALU.mult, ALU.mult
-            )
+        ds = [scatter("ds_%d" % t, n1_l, y[t]) for t in range(TILES)]
 
-        for t in range(TILES):
-            ds.append(scatter("ds_%d" % t, n1_l, y[t]))
-            if 0 < t < TILES - 1:
-                make_z(t - 1, 0, S)
-        make_z(TILES - 2, 0, S)
-        make_z(TILES - 1, 0, HEAD)
-        make_z(TILES - 1, HEAD, S)
+        def make_z(name, a):
+            rows = tile(name, [P, TILES, HEAD], BF16, "z_rows")
+            for t in range(TILES):
+                nc.vector.scalar_tensor_tensor(
+                    rows[:, t, :], ds[t][:, a : a + HEAD], gs_c[:, t : t + 1], sg[t][:, a : a + HEAD], ALU.mult, ALU.mult
+                )
+            return rows[:].rearrange("p t c -> p c t")
 
-        pieces = [(0, HEAD), (HEAD, 2 * HEAD), (2 * HEAD, S)]
-        z_q = []
-        for i, (a, b) in enumerate(pieces):
-            grouped = tile("z_g%d" % i, [P, b - a, PACK], BF16)
-            src = z_rows[:, :, a:b].rearrange("p t c -> p c t")
-            if i == 0:
-                nc.vector.tensor_copy(grouped[:], src)
-            else:
-                nc.scalar.copy(grouped[:], src)
-            z_q.append(grouped)
-
-        h2 = [tile("h2_%d" % t, [P, S], F32) for t in range(TILES)]
-        ds2 = [tile("ds2_%d" % t, [P, WIDE], F32) for t in range(TILES)]
-
-        def second_product(acc, t, codes, plane):
+        def second_product(bank_number, t, a, codes, plane):
+            bank = psum.tile([P, S], F32, name="bank%d" % bank_number)
             for half in range(2):
                 m = slice(half * P, (half + 1) * P)
                 sm = slice(t * 2 * P + half * P, t * 2 * P + (half + 1) * P)
                 nc.tensor.matmul_mx(
-                    out=acc, lhsT=dw_dealt[t][:, m].bitcast(FP8X4), lhsT_scale=ds_plane[:, sm],
+                    out=bank[:, 0:HEAD], lhsT=dw_dealt[t][:, m].bitcast(FP8X4), lhsT_scale=ds_plane[:, sm],
                     rhs=codes[:].bitcast(FP8X4), rhs_scale=plane[:], start=(half == 0), stop=(half == 1),
                 )
+            nc.scalar.activation(out=h2[t][:, a : a + HEAD], in_=bank[:, 0:HEAD], func=ACT.Copy, scale=0.0625)
 
-        codes, plane = quantize("z0", z_q[0][:].rearrange("p c t -> p (c t)"), HEAD)
+        h2 = [tile("h2_%d" % t, [P, S], F32) for t in range(TILES)]
+
+        z_first = tile("z_first", [P, HEAD, PACK], BF16)
+        nc.vector.tensor_copy(z_first[:], make_z("z_rows_first", 0))
+        codes, plane = quantize("z_first", z_first[:].rearrange("p c t -> p (c t)"), HEAD, "chain")
         for t in range(TILES):
-            bank = psum.tile([P, S], F32, name="bank%d" % t)
-            second_product(bank[:, 0:HEAD], t, codes, plane)
-            nc.scalar.activation(out=h2[t][:, 0:HEAD], in_=bank[:, 0:HEAD], func=ACT.Copy, scale=0.0625)
-        rest = [quantize("z%d" % i, z_q[i][:].rearrange("p c t -> p (c t)"), b - a) for i, (a, b) in enumerate(pieces) if i]
+            second_product(t, t, 0, codes, plane)
+        rows = make_z("z_rows_second", HEAD)
+        z_second = tile("z_second", [P, HEAD, PACK], BF16, "chain")
+        nc.scalar.copy(z_second[:], rows)
+        codes, plane = quantize("z_second", z_second[:].rearrange("p c t -> p (c t)"), HEAD)
+        ds2 = [tile("ds2_%d" % t, [P, WIDE], F32, "chain" if t == 2 else "") for t in range(TILES)]
         for t in range(TILES):
             nc.vector.tensor_copy(ds2[t][:].indirect(cols(n3_l, 0, HEAD)), h2[t][:, 0:HEAD])
         for t in range(TILES):
-            bank = psum.tile([P, S], F32, name="bank%d" % (TILES + t))
-            for (a, b), (codes, plane) in zip(pieces[1:], rest):
-                second_product(bank[:, a:b], t, codes, plane)
-            nc.scalar.activation(out=h2[t][:, HEAD:S], in_=bank[:, HEAD:S], func=ACT.Copy, scale=0.0625)
+            second_product(TILES + t, t, HEAD, codes, plane)
 
         def open_bank(number):
             return psum.tile([P, S], F32, name="bank%d" % number)
@@ -242,14 +224,12 @@ def tile_picked_dthzaesndsndtwin_none_p_kernel(
             nc.scalar.activation(out=dst[:], in_=src[:], func=func, scale=scale)
             return dst
 
-        h2_turned, diff_bank, st_bank = [], [], []
+        h2_neg, h2_turned, st_bank = [], [], []
         for t in range(TILES):
-            h2_neg = leave("h2_neg%d" % t, h2[t], ACT.Copy, -1.0)
+            h2_neg.append(leave("h2_neg%d" % t, h2[t], ACT.Copy, -1.0))
             bank = open_bank(t)
             add_turned(bank, h2[t], first=True, last=True)
             h2_turned.append(leave("h2_turned%d" % t, bank, ACT.Copy, 1.0))
-            diff_bank.append(open_bank(TILES + t))
-            add_turned(diff_bank[t], h2_neg, first=True)
             st_bank.append(open_bank(t))
             add_turned(st_bank[t], h2_turned[t], first=True)
 
@@ -257,8 +237,10 @@ def tile_picked_dthzaesndsndtwin_none_p_kernel(
         st, out_bank = [], []
         for t in range(TILES):
             nc.vector.tensor_copy(ds2[t][:].indirect(cols(n3_l, HEAD, S)), h2[t][:, HEAD:S])
-            add_turned(diff_bank[t], ds2[t], last=True)
-            gain = leave("gain%d" % t, diff_bank[t], ACT.Relu, 1.0)
+            diff_bank = open_bank(TILES + t % 2)
+            add_turned(diff_bank, h2_neg[t], first=True)
+            add_turned(diff_bank, ds2[t], last=True)
+            gain = leave("gain%d" % t, diff_bank, ACT.Relu, 1.0)
             add_turned(st_bank[t], gain, last=True)
             st.append(leave("st%d" % t, st_bank[t], ACT.Copy, 1.0))
             if t < TILES - 1:
@@ -268,14 +250,14 @@ def tile_picked_dthzaesndsndtwin_none_p_kernel(
         for t in range(TILES):
             ds3 = scatter("ds3_%d" % t, n4_l, st[t])
             if t < TILES - 1:
-                bank = open_bank(TILES + t)
+                bank = open_bank(TILES + t % 2)
                 add_turned(bank, ds3, first=True, last=True)
                 add_turned(out_bank[t], leave("ds3_neg%d" % t, bank, ACT.Copy, -1.0), last=True)
                 res = leave("res%d" % t, out_bank[t], ACT.Copy, 1.0)
-                nc.sync.dma_start(out_rows[t], res[:])
+                nc.scalar.dma_start(out_rows[t], res[:])
             else:
                 res = tile("res%d" % t, [P, S], F32)
-                for a, queue in ((0, nc.sync), (S // 2, nc.scalar)):
+                for a in range(0, S, S // 2):
                     half = slice(a, a + S // 2)
                     nc.vector.tensor_tensor(res[:, half], st[t][:, half], ds3[:, half], ALU.subtract)
-                    queue.dma_start(out_rows[t][:, :, half], res[:, half])
+                    nc.sync.dma_start(out_rows[t][:, :, half], res[:, half])

@@ -13,13 +13,17 @@ FP8X4 = mybir.dt.float8_e4m3fn_x4
 ALU = mybir.AluOpType
 ACT = mybir.ActivationFunctionType
 
+K, T, S, H, G = 512, 1024, 512, 512, 2048
 P = 128
 PACK = 4
-K, T, S, H, G = 512, 1024, 512, 512, 2048
+GROUP = 16
+BLOCK_PARTITIONS = 8
+QUADRANT = 32
 TILES = H // P
-RUN = 8
-HEAD = 256
+PIECE = 8
+HALF = S // 2
 WIDE = 2 * S
+VECTOR_DEALT = 2
 
 FLOPS = 2 * 2 * K * H * S + 2 * 2 * K * H * S
 
@@ -33,22 +37,28 @@ def tile_picked_dthzaesndsndtwin_none_p_kernel(
         keep = ctx.enter_context(tc.tile_pool(name="keep", bufs=1))
         psum = ctx.enter_context(tc.psum_pool(name="psum", bufs=1))
 
-        def tile(name, shape, dtype, tag=""):
-            return keep.tile(shape, dtype, name=name, tag=tag or name, align_bytes=64)
+        def tile(name, shape, dtype, after=""):
+            return keep.tile(shape, dtype, name=name, tag=after or name, align_bytes=64)
+
+        def open_bank(number):
+            return psum.tile([P, S], F32, name="bank%d" % number)
+
+        def entries(list_tile, first, end):
+            return list_tile[:, first // GROUP : end // GROUP]
 
         def load_list(name, src):
-            dst = lists.tile([P, S // 16], U16, name=name)
+            dst = lists.tile([P, S // GROUP], U16, name=name)
             nc.sync.dma_start(dst[:], src)
             return dst
 
         def load_scales(name, scales, width):
             dst = tile(name, [P, width], U8)
             nc.gpsimd.memset(dst[:].bitcast(I32), 0)
-            nc.sync.dma_start(dst[0:P:8, :].bitcast(I32), scales[0].bitcast(I32))
+            nc.sync.dma_start(dst[0:P:BLOCK_PARTITIONS, :].bitcast(I32), scales[0].bitcast(I32))
             return dst
 
-        def load_words(name, words, width, tag=""):
-            dst = tile(name, [P, width], U32, tag)
+        def load_words(name, words, width):
+            dst = tile(name, [P, width], U32)
             nc.sync.dma_start(dst[:].bitcast(I32), words[0].rearrange("p n t -> p (n t)").bitcast(I32))
             return dst
 
@@ -57,207 +67,209 @@ def tile_picked_dthzaesndsndtwin_none_p_kernel(
             nc.sync.dma_start(dst[:], w.rearrange("(p j) c -> p j c", j=PACK))
             return dst
 
-        def load_column(name, v, tag):
-            dst = tile(name, [P, TILES], F32, tag)
-            nc.sync.dma_start(dst[:], v.rearrange("(p t) o -> p (t o)", t=TILES))
+        def load_row_values(name, values, after):
+            dst = tile(name, [P, TILES], F32, after)
+            nc.sync.dma_start(dst[:], values.rearrange("(p t) o -> p (t o)", t=TILES))
             return dst
 
-        def cols(lst, a, b):
-            return lst[:, a // 16 : b // 16]
-
         offs_l = load_list("offs_l", offs)
-        xs_win = load_scales("xs_win", x_scales, T)
+        x_scale_table = load_scales("x_scale_table", x_scales, T)
         hz_l = load_list("hz_l", hz)
         ka_l = load_list("ka_l", ka)
-        ds_win = load_scales("ds_win", d_scales, G)
+        d_scale_table = load_scales("d_scale_table", d_scales, G)
         kb_l = load_list("kb_l", kb)
         w1_raw = load_weight("w1_raw", w1)
         w2_raw = load_weight("w2_raw", w2)
-        xw_win = load_words("xw_win", x_words, T)
+        x_word_table = load_words("x_word_table", x_words, T)
         n1_l = load_list("n1_l", n1)
         n2_l = load_list("n2_l", n2)
         n3_l = load_list("n3_l", n3)
         n4_l = load_list("n4_l", n4)
-        dw_win = load_words("dw_win", d_words, G)
+        d_word_table = load_words("d_word_table", d_words, G)
 
-        s_pick = tile("s_pick", [P, 4 * S], U8)
-        nc.vector.tensor_copy(s_pick[:, 0:S], xs_win[:].indirect(offs_l[:]))
-        nc.vector.tensor_copy(s_pick[:, S : 2 * S], xs_win[:].indirect(hz_l[:]))
-        nc.vector.tensor_copy(s_pick[:, 2 * S : 3 * S], ds_win[:].indirect(ka_l[:]))
-        nc.vector.tensor_copy(s_pick[:, 3 * S : 4 * S], ds_win[:].indirect(kb_l[:]))
-        xs_plane = tile("xs_plane", [P, 4 * S], U8)
-        nc.vector.memset(xs_plane[:].bitcast(I32), 0)
-        for r in range(4):
-            nc.sync.dma_start(xs_plane[r:P:32, :].bitcast(I32), s_pick[8 * r : P : 32, :].bitcast(I32))
+        picked_scales = tile("picked_scales", [P, 4 * S], U8)
+        nc.vector.tensor_copy(picked_scales[:, 0:S], x_scale_table[:].indirect(offs_l[:]))
+        nc.vector.tensor_copy(picked_scales[:, S : 2 * S], x_scale_table[:].indirect(hz_l[:]))
+        nc.vector.tensor_copy(picked_scales[:, 2 * S : 3 * S], d_scale_table[:].indirect(ka_l[:]))
+        nc.vector.tensor_copy(picked_scales[:, 3 * S : 4 * S], d_scale_table[:].indirect(kb_l[:]))
+        placed_scales = tile("placed_scales", [P, 4 * S], U8)
+        nc.vector.memset(placed_scales[:].bitcast(I32), 0)
+        for r in range(QUADRANT // BLOCK_PARTITIONS):
+            nc.sync.dma_start(
+                placed_scales[r:P:QUADRANT, :].bitcast(I32),
+                picked_scales[BLOCK_PARTITIONS * r : P : QUADRANT, :].bitcast(I32),
+            )
 
-        sl_c = load_column("sl_c", sl, "xs_win")
-        th_c = load_column("th_c", th, "ds_win")
-        gs_c = load_column("gs_c", gs, "s_pick")
+        sl_rows = load_row_values("sl_rows", sl, "x_scale_table")
+        th_rows = load_row_values("th_rows", th, "d_scale_table")
+        gs_rows = load_row_values("gs_rows", gs, "picked_scales")
 
-        ident = tile("ident", [P, P], F32)
-        make_identity(nc, ident[:])
+        identity = tile("identity", [P, P], F32)
+        make_identity(nc, identity[:])
 
-        def quantize(name, grouped, width, tag=""):
-            codes = tile(name + "_codes", [P, width], U32, tag)
-            plane = tile(name + "_plane", [P, width], U8)
-            nc.vector.quantize_mx(out=codes[:].bitcast(FP8X4), scales=plane[:], in_=grouped)
-            return codes, plane
+        def quantize(name, grouped, width, after=""):
+            codes = tile(name + "_codes", [P, width], U32, after)
+            scales = tile(name + "_scales", [P, width], U8)
+            nc.vector.quantize_mx(out=codes[:].bitcast(FP8X4), scales=scales[:], in_=grouped)
+            return codes, scales
 
-        def quantize_weight_half(name, raw, half):
-            grouped = tile(name, [P, 2, P, PACK], BF16)
+        def quantize_weight(name, raw):
+            grouped = tile(name + "_grouped", [P, TILES, P, PACK], BF16)
             nc.scalar.copy(
                 grouped[:].rearrange("p t m j -> p m t j"),
-                raw[:].rearrange("p j (m t) -> p m t j", t=TILES)[:, :, 2 * half : 2 * half + 2, :],
+                raw[:].rearrange("p j (m t) -> p m t j", t=TILES),
             )
-            return quantize(name, grouped[:].rearrange("p t m j -> p (t m j)"), 2 * P)
+            return quantize(name, grouped[:].rearrange("p t m j -> p (t m j)"), H)
 
-        w1_q = [quantize_weight_half("w1_%d" % half, w1_raw, half) for half in range(2)]
-        x_offs = tile("x_offs", [P, S], U32)
-        nc.vector.tensor_copy(x_offs[:], xw_win[:].indirect(offs_l[:]))
-        x_hz = tile("x_hz", [P, S], U32)
-        nc.vector.tensor_copy(x_hz[:], xw_win[:].indirect(hz_l[:]))
-        w2_q = [quantize_weight_half("w2_%d" % half, w2_raw, half) for half in range(2)]
+        w1_codes, w1_scales = quantize_weight("w1", w1_raw)
+        x_by_offs = tile("x_by_offs", [P, S], U32)
+        nc.vector.tensor_copy(x_by_offs[:], x_word_table[:].indirect(offs_l[:]))
+        x_by_hz = tile("x_by_hz", [P, S], U32)
+        nc.vector.tensor_copy(x_by_hz[:], x_word_table[:].indirect(hz_l[:]))
+        w2_codes, w2_scales = quantize_weight("w2", w2_raw)
 
         bias = tile("bias", [P, TILES], F32)
-        nc.vector.scalar_tensor_tensor(bias[:], sl_c[:], -1.0, th_c[:], ALU.mult, ALU.mult)
+        sl_th = tile("sl_th", [P, TILES], F32)
+        nc.gpsimd.tensor_tensor(sl_th[:], sl_rows[:], th_rows[:], ALU.mult)
+        nc.gpsimd.tensor_scalar(bias[:], sl_th[:], -1.0, 0.0, ALU.mult, ALU.add)
 
-        dw_pick = tile("dw_pick", [P, 2 * H], U32)
-        nc.vector.tensor_copy(dw_pick[:, 0:H], dw_win[:].indirect(ka_l[:]))
-        nc.vector.tensor_copy(dw_pick[:, H : 2 * H], dw_win[:].indirect(kb_l[:]))
+        d_picked = tile("d_picked", [P, 2 * H], U32)
+        nc.vector.tensor_copy(d_picked[:, 0:H], d_word_table[:].indirect(ka_l[:]))
+        nc.vector.tensor_copy(d_picked[:, H : 2 * H], d_word_table[:].indirect(kb_l[:]))
 
-        ds_plane = tile("ds_plane", [P, 2 * H], U8)
+        d_dealt_scales = tile("d_dealt_scales", [P, 2 * H], U8)
         nc.vector.tensor_copy(
-            ds_plane[:].bitcast(I32).rearrange("p (t a w) -> p t a w", t=TILES, w=RUN // 4),
-            xs_plane[:, 2 * S : 4 * S].bitcast(I32).rearrange("p (a t w) -> p t a w", t=TILES, w=RUN // 4),
+            d_dealt_scales[:].bitcast(I32).rearrange("p (t a w) -> p t a w", t=TILES, w=PIECE // PACK),
+            placed_scales[:, 2 * S : 4 * S].bitcast(I32).rearrange("p (a t w) -> p t a w", t=TILES, w=PIECE // PACK),
         )
-
-        dw_dealt = []
-        for t in range(TILES):
-            dealt = tile("dw_dealt%d" % t, [P, 2 * P], U32)
-            nc.sync.dma_start(
-                dealt[:].bitcast(I32).rearrange("p (a w) -> p a w", w=RUN),
-                dw_pick[:].bitcast(I32).rearrange("p (a t w) -> p t a w", t=TILES, w=RUN)[:, t],
-            )
-            dw_dealt.append(dealt)
 
         y, sg = [], []
         for t in range(TILES):
-            bank = psum.tile([P, S], F32, name="bank%d" % t)
-            m = slice(t % 2 * P, (t % 2 + 1) * P)
-            w1_codes, w1_plane = w1_q[t // 2]
-            w2_codes, w2_plane = w2_q[t // 2]
+            bank = open_bank(t)
+            m = slice(t * P, (t + 1) * P)
             nc.tensor.matmul_mx(
-                out=bank[:], lhsT=w1_codes[:, m].bitcast(FP8X4), lhsT_scale=w1_plane[:, m],
-                rhs=x_offs[:].bitcast(FP8X4), rhs_scale=xs_plane[:, 0:S], start=True, stop=False,
+                out=bank[:], lhsT=w1_codes[:, m].bitcast(FP8X4), lhsT_scale=w1_scales[:, m],
+                rhs=x_by_offs[:].bitcast(FP8X4), rhs_scale=placed_scales[:, 0:S], start=True, stop=False,
             )
             nc.tensor.matmul_mx(
-                out=bank[:], lhsT=w2_codes[:, m].bitcast(FP8X4), lhsT_scale=w2_plane[:, m],
-                rhs=x_hz[:].bitcast(FP8X4), rhs_scale=xs_plane[:, S : 2 * S], start=False, stop=True,
+                out=bank[:], lhsT=w2_codes[:, m].bitcast(FP8X4), lhsT_scale=w2_scales[:, m],
+                rhs=x_by_hz[:].bitcast(FP8X4), rhs_scale=placed_scales[:, S : 2 * S], start=False, stop=True,
             )
-            y_t = tile("y%d" % t, [P, S], F32)
-            nc.scalar.copy(y_t[:], bank[:])
-            y.append(y_t)
+            y.append(tile("y%d" % t, [P, S], F32))
+            nc.scalar.copy(y[t][:], bank[:])
         for t in range(TILES):
-            sg_t = tile("sg%d" % t, [P, S], F32)
-            for a in range(0, S, S // 2):
+            sg.append(tile("sg%d" % t, [P, S], F32))
+            for a in range(0, S, HALF):
                 nc.scalar.activation(
-                    out=sg_t[:, a : a + S // 2], in_=y[t][:].indirect(cols(n2_l, a, a + S // 2)),
-                    func=ACT.Sigmoid, scale=sl_c[:, t : t + 1], bias=bias[:, t : t + 1],
+                    out=sg[t][:, a : a + HALF], in_=y[t][:].indirect(entries(n2_l, a, a + HALF)),
+                    func=ACT.Sigmoid, scale=sl_rows[:, t : t + 1], bias=bias[:, t : t + 1],
                 )
-            sg.append(sg_t)
 
-        def scatter(name, lst, src):
-            win = tile(name, [P, WIDE], F32)
-            nc.vector.tensor_copy(win[:].indirect(lst[:]), src[:])
-            return win
+        def scatter(name, list_tile, src):
+            window = tile(name, [P, WIDE], F32)
+            nc.vector.tensor_copy(window[:].indirect(list_tile[:]), src[:])
+            return window
 
         ds = [scatter("ds_%d" % t, n1_l, y[t]) for t in range(TILES)]
 
+        pieces = d_picked[:].bitcast(I32).rearrange("p (a t w) -> p t a w", t=TILES, w=PIECE)
+        early = tile("d_dealt_early", [P, VECTOR_DEALT, 2 * P], U32, "y0")
+        nc.vector.tensor_copy(
+            early[:].bitcast(I32).rearrange("p t (a w) -> p t a w", w=PIECE), pieces[:, 0:VECTOR_DEALT]
+        )
+        d_dealt = [early[:, t, :] for t in range(VECTOR_DEALT)]
+        for t in range(VECTOR_DEALT, TILES):
+            late = tile("d_dealt_late%d" % t, [P, 2 * P], U32)
+            nc.sync.dma_start(late[:].bitcast(I32).rearrange("p (a w) -> p a w", w=PIECE), pieces[:, t])
+            d_dealt.append(late[:])
+
         def make_z(name, a):
-            rows = tile(name, [P, TILES, HEAD], BF16, "z_rows")
+            rows = tile(name, [P, TILES, HALF], BF16, "z_rows")
             for t in range(TILES):
                 nc.vector.scalar_tensor_tensor(
-                    rows[:, t, :], ds[t][:, a : a + HEAD], gs_c[:, t : t + 1], sg[t][:, a : a + HEAD], ALU.mult, ALU.mult
+                    rows[:, t, :], ds[t][:, a : a + HALF], gs_rows[:, t : t + 1], sg[t][:, a : a + HALF],
+                    ALU.mult, ALU.mult,
                 )
             return rows[:].rearrange("p t c -> p c t")
 
-        def second_product(bank_number, t, a, codes, plane):
-            bank = psum.tile([P, S], F32, name="bank%d" % bank_number)
-            for half in range(2):
-                m = slice(half * P, (half + 1) * P)
-                sm = slice(t * 2 * P + half * P, t * 2 * P + (half + 1) * P)
+        def second_product(bank_number, t, a, z_codes, z_scales):
+            bank = open_bank(bank_number)
+            for which in range(2):
+                m = slice(which * P, (which + 1) * P)
+                m_scales = slice((2 * t + which) * P, (2 * t + which + 1) * P)
                 nc.tensor.matmul_mx(
-                    out=bank[:, 0:HEAD], lhsT=dw_dealt[t][:, m].bitcast(FP8X4), lhsT_scale=ds_plane[:, sm],
-                    rhs=codes[:].bitcast(FP8X4), rhs_scale=plane[:], start=(half == 0), stop=(half == 1),
+                    out=bank[:, 0:HALF], lhsT=d_dealt[t][:, m].bitcast(FP8X4), lhsT_scale=d_dealt_scales[:, m_scales],
+                    rhs=z_codes[:].bitcast(FP8X4), rhs_scale=z_scales[:], start=(which == 0), stop=(which == 1),
                 )
-            nc.scalar.activation(out=h2[t][:, a : a + HEAD], in_=bank[:, 0:HEAD], func=ACT.Copy, scale=0.0625)
+            nc.scalar.activation(out=h2[t][:, a : a + HALF], in_=bank[:, 0:HALF], func=ACT.Copy, scale=0.0625)
 
         h2 = [tile("h2_%d" % t, [P, S], F32) for t in range(TILES)]
 
-        z_first = tile("z_first", [P, HEAD, PACK], BF16)
+        z_first = tile("z_first", [P, HALF, PACK], BF16)
         nc.vector.tensor_copy(z_first[:], make_z("z_rows_first", 0))
-        codes, plane = quantize("z_first", z_first[:].rearrange("p c t -> p (c t)"), HEAD, "chain")
+        first_codes, first_scales = quantize("z_first", z_first[:].rearrange("p c t -> p (c t)"), HALF, "z_halves")
         for t in range(TILES):
-            second_product(t, t, 0, codes, plane)
-        rows = make_z("z_rows_second", HEAD)
-        z_second = tile("z_second", [P, HEAD, PACK], BF16, "chain")
-        nc.scalar.copy(z_second[:], rows)
-        codes, plane = quantize("z_second", z_second[:].rearrange("p c t -> p (c t)"), HEAD)
-        ds2 = [tile("ds2_%d" % t, [P, WIDE], F32, "chain" if t == 2 else "") for t in range(TILES)]
+            second_product(t, t, 0, first_codes, first_scales)
+        z_rows_second = make_z("z_rows_second", HALF)
+        z_second = tile("z_second", [P, HALF, PACK], BF16, "z_halves")
+        nc.scalar.copy(z_second[:], z_rows_second)
+        second_codes, second_scales = quantize("z_second", z_second[:].rearrange("p c t -> p (c t)"), HALF)
+        ds2_after = ("", "", "z_rows", "z_halves")
+        ds2 = [tile("ds2_%d" % t, [P, WIDE], F32, ds2_after[t]) for t in range(TILES)]
         for t in range(TILES):
-            nc.vector.tensor_copy(ds2[t][:].indirect(cols(n3_l, 0, HEAD)), h2[t][:, 0:HEAD])
+            nc.vector.tensor_copy(ds2[t][:].indirect(entries(n3_l, 0, HALF)), h2[t][:, 0:HALF])
         for t in range(TILES):
-            second_product(TILES + t, t, HEAD, codes, plane)
-
-        def open_bank(number):
-            return psum.tile([P, S], F32, name="bank%d" % number)
+            second_product(TILES + t, t, HALF, second_codes, second_scales)
 
         def add_turned(bank, term, first=False, last=False):
             for b in range(0, S, P):
                 nc.tensor.matmul(
-                    bank[:, b : b + P], term[:, b : b + P], ident[:],
+                    bank[:, b : b + P], term[:, b : b + P], identity[:],
                     start=(first and b == 0), stop=(last and b == S - P), is_transpose=True,
                 )
 
-        def leave(name, src, func, scale):
+        def through_scalar(name, src, func, scale):
             dst = tile(name, [P, S], F32)
             nc.scalar.activation(out=dst[:], in_=src[:], func=func, scale=scale)
             return dst
 
-        h2_neg, h2_turned, st_bank = [], [], []
+        def spare_bank(t):
+            return open_bank(TILES + t % 2)
+
+        h2_negated, h2_turned, st_bank = [], [], []
         for t in range(TILES):
-            h2_neg.append(leave("h2_neg%d" % t, h2[t], ACT.Copy, -1.0))
+            h2_negated.append(through_scalar("h2_negated%d" % t, h2[t], ACT.Copy, -1.0))
             bank = open_bank(t)
             add_turned(bank, h2[t], first=True, last=True)
-            h2_turned.append(leave("h2_turned%d" % t, bank, ACT.Copy, 1.0))
+            h2_turned.append(through_scalar("h2_turned%d" % t, bank, ACT.Copy, 1.0))
             st_bank.append(open_bank(t))
             add_turned(st_bank[t], h2_turned[t], first=True)
 
-        out_rows = out.rearrange("(a t w) c -> t a w c", t=TILES, w=RUN)
+        out_rows = out.rearrange("(a t w) c -> t a w c", t=TILES, w=PIECE)
         st, out_bank = [], []
         for t in range(TILES):
-            nc.vector.tensor_copy(ds2[t][:].indirect(cols(n3_l, HEAD, S)), h2[t][:, HEAD:S])
-            diff_bank = open_bank(TILES + t % 2)
-            add_turned(diff_bank, h2_neg[t], first=True)
-            add_turned(diff_bank, ds2[t], last=True)
-            gain = leave("gain%d" % t, diff_bank, ACT.Relu, 1.0)
-            add_turned(st_bank[t], gain, last=True)
-            st.append(leave("st%d" % t, st_bank[t], ACT.Copy, 1.0))
+            nc.vector.tensor_copy(ds2[t][:].indirect(entries(n3_l, HALF, S)), h2[t][:, HALF:S])
+            bank = spare_bank(t)
+            add_turned(bank, h2_negated[t], first=True)
+            add_turned(bank, ds2[t], last=True)
+            excess_turned = through_scalar("excess_turned%d" % t, bank, ACT.Relu, 1.0)
+            add_turned(st_bank[t], excess_turned, last=True)
+            st.append(through_scalar("st%d" % t, st_bank[t], ACT.Copy, 1.0))
             if t < TILES - 1:
                 out_bank.append(open_bank(t))
                 add_turned(out_bank[t], h2_turned[t], first=True)
-                add_turned(out_bank[t], gain)
+                add_turned(out_bank[t], excess_turned)
         for t in range(TILES):
             ds3 = scatter("ds3_%d" % t, n4_l, st[t])
             if t < TILES - 1:
-                bank = open_bank(TILES + t % 2)
+                bank = spare_bank(t)
                 add_turned(bank, ds3, first=True, last=True)
-                add_turned(out_bank[t], leave("ds3_neg%d" % t, bank, ACT.Copy, -1.0), last=True)
-                res = leave("res%d" % t, out_bank[t], ACT.Copy, 1.0)
-                nc.scalar.dma_start(out_rows[t], res[:])
+                add_turned(out_bank[t], through_scalar("ds3_negated_turned%d" % t, bank, ACT.Copy, -1.0), last=True)
+                result = through_scalar("result%d" % t, out_bank[t], ACT.Copy, 1.0)
+                nc.scalar.dma_start(out_rows[t], result[:])
             else:
-                res = tile("res%d" % t, [P, S], F32)
-                for a in range(0, S, S // 2):
-                    half = slice(a, a + S // 2)
-                    nc.vector.tensor_tensor(res[:, half], st[t][:, half], ds3[:, half], ALU.subtract)
-                    nc.sync.dma_start(out_rows[t][:, :, half], res[:, half])
+                result = tile("result%d" % t, [P, S], F32)
+                for a in range(0, S, HALF):
+                    half = slice(a, a + HALF)
+                    nc.vector.tensor_tensor(result[:, half], st[t][:, half], ds3[:, half], ALU.subtract)
+                    nc.sync.dma_start(out_rows[t][:, :, half], result[:, half])

from contextlib import ExitStack

import concourse.mybir as mybir
from concourse.masks import make_identity

F32 = mybir.dt.float32
BF16 = mybir.dt.bfloat16
I32 = mybir.dt.int32
U32 = mybir.dt.uint32
U16 = mybir.dt.uint16
U8 = mybir.dt.uint8
FP8X4 = mybir.dt.float8_e4m3fn_x4
ALU = mybir.AluOpType
ACT = mybir.ActivationFunctionType

K, T, S, H, G = 512, 1024, 512, 512, 2048
P = 128
PACK = 4
GROUP = 16
BLOCK_PARTITIONS = 8
QUADRANT = 32
TILES = H // P
PIECE = 8
HALF = S // 2
WIDE = 2 * S
VECTOR_DEALT = 2

FLOPS = 2 * 2 * K * H * S + 2 * 2 * K * H * S


def tile_picked_dthzaesndsndtwin_none_p_kernel(
    tc, x_words, x_scales, w1, w2, sl, th, gs, d_words, d_scales, offs, hz, n1, n2, ka, kb, n3, n4, out
):
    nc = tc.nc
    with ExitStack() as ctx:
        lists = ctx.enter_context(tc.tile_pool(name="lists", bufs=1))
        keep = ctx.enter_context(tc.tile_pool(name="keep", bufs=1))
        psum = ctx.enter_context(tc.psum_pool(name="psum", bufs=1))

        def tile(name, shape, dtype, after=""):
            return keep.tile(shape, dtype, name=name, tag=after or name, align_bytes=64)

        def open_bank(number):
            return psum.tile([P, S], F32, name="bank%d" % number)

        def entries(list_tile, first, end):
            return list_tile[:, first // GROUP : end // GROUP]

        def load_list(name, src):
            dst = lists.tile([P, S // GROUP], U16, name=name)
            nc.sync.dma_start(dst[:], src)
            return dst

        def load_scales(name, scales, width):
            dst = tile(name, [P, width], U8)
            nc.gpsimd.memset(dst[:].bitcast(I32), 0)
            nc.sync.dma_start(dst[0:P:BLOCK_PARTITIONS, :].bitcast(I32), scales[0].bitcast(I32))
            return dst

        def load_words(name, words, width):
            dst = tile(name, [P, width], U32)
            nc.sync.dma_start(dst[:].bitcast(I32), words[0].rearrange("p n t -> p (n t)").bitcast(I32))
            return dst

        def load_weight(name, w):
            dst = tile(name, [P, PACK, H], F32)
            nc.sync.dma_start(dst[:], w.rearrange("(p j) c -> p j c", j=PACK))
            return dst

        def load_row_values(name, values, after):
            dst = tile(name, [P, TILES], F32, after)
            nc.sync.dma_start(dst[:], values.rearrange("(p t) o -> p (t o)", t=TILES))
            return dst

        offs_l = load_list("offs_l", offs)
        x_scale_table = load_scales("x_scale_table", x_scales, T)
        hz_l = load_list("hz_l", hz)
        ka_l = load_list("ka_l", ka)
        d_scale_table = load_scales("d_scale_table", d_scales, G)
        kb_l = load_list("kb_l", kb)
        w1_raw = load_weight("w1_raw", w1)
        w2_raw = load_weight("w2_raw", w2)
        x_word_table = load_words("x_word_table", x_words, T)
        n1_l = load_list("n1_l", n1)
        n2_l = load_list("n2_l", n2)
        n3_l = load_list("n3_l", n3)
        n4_l = load_list("n4_l", n4)
        d_word_table = load_words("d_word_table", d_words, G)

        picked_scales = tile("picked_scales", [P, 4 * S], U8)
        nc.vector.tensor_copy(picked_scales[:, 0:S], x_scale_table[:].indirect(offs_l[:]))
        nc.vector.tensor_copy(picked_scales[:, S : 2 * S], x_scale_table[:].indirect(hz_l[:]))
        nc.vector.tensor_copy(picked_scales[:, 2 * S : 3 * S], d_scale_table[:].indirect(ka_l[:]))
        nc.vector.tensor_copy(picked_scales[:, 3 * S : 4 * S], d_scale_table[:].indirect(kb_l[:]))
        placed_scales = tile("placed_scales", [P, 4 * S], U8)
        nc.vector.memset(placed_scales[:].bitcast(I32), 0)
        for r in range(QUADRANT // BLOCK_PARTITIONS):
            nc.sync.dma_start(
                placed_scales[r:P:QUADRANT, :].bitcast(I32),
                picked_scales[BLOCK_PARTITIONS * r : P : QUADRANT, :].bitcast(I32),
            )

        sl_rows = load_row_values("sl_rows", sl, "x_scale_table")
        th_rows = load_row_values("th_rows", th, "d_scale_table")
        gs_rows = load_row_values("gs_rows", gs, "picked_scales")

        identity = tile("identity", [P, P], F32)
        make_identity(nc, identity[:])

        def quantize(name, grouped, width, after=""):
            codes = tile(name + "_codes", [P, width], U32, after)
            scales = tile(name + "_scales", [P, width], U8)
            nc.vector.quantize_mx(out=codes[:].bitcast(FP8X4), scales=scales[:], in_=grouped)
            return codes, scales

        def quantize_weight(name, raw):
            grouped = tile(name + "_grouped", [P, TILES, P, PACK], BF16)
            nc.scalar.copy(
                grouped[:].rearrange("p t m j -> p m t j"),
                raw[:].rearrange("p j (m t) -> p m t j", t=TILES),
            )
            return quantize(name, grouped[:].rearrange("p t m j -> p (t m j)"), H)

        w1_codes, w1_scales = quantize_weight("w1", w1_raw)
        x_by_offs = tile("x_by_offs", [P, S], U32)
        nc.vector.tensor_copy(x_by_offs[:], x_word_table[:].indirect(offs_l[:]))
        x_by_hz = tile("x_by_hz", [P, S], U32)
        nc.vector.tensor_copy(x_by_hz[:], x_word_table[:].indirect(hz_l[:]))
        w2_codes, w2_scales = quantize_weight("w2", w2_raw)

        bias = tile("bias", [P, TILES], F32)
        sl_th = tile("sl_th", [P, TILES], F32)
        nc.gpsimd.tensor_tensor(sl_th[:], sl_rows[:], th_rows[:], ALU.mult)
        nc.gpsimd.tensor_scalar(bias[:], sl_th[:], -1.0, 0.0, ALU.mult, ALU.add)

        d_picked = tile("d_picked", [P, 2 * H], U32)
        nc.vector.tensor_copy(d_picked[:, 0:H], d_word_table[:].indirect(ka_l[:]))
        nc.vector.tensor_copy(d_picked[:, H : 2 * H], d_word_table[:].indirect(kb_l[:]))

        d_dealt_scales = tile("d_dealt_scales", [P, 2 * H], U8)
        nc.vector.tensor_copy(
            d_dealt_scales[:].bitcast(I32).rearrange("p (t a w) -> p t a w", t=TILES, w=PIECE // PACK),
            placed_scales[:, 2 * S : 4 * S].bitcast(I32).rearrange("p (a t w) -> p t a w", t=TILES, w=PIECE // PACK),
        )

        y, sg = [], []
        for t in range(TILES):
            bank = open_bank(t)
            m = slice(t * P, (t + 1) * P)
            nc.tensor.matmul_mx(
                out=bank[:], lhsT=w1_codes[:, m].bitcast(FP8X4), lhsT_scale=w1_scales[:, m],
                rhs=x_by_offs[:].bitcast(FP8X4), rhs_scale=placed_scales[:, 0:S], start=True, stop=False,
            )
            nc.tensor.matmul_mx(
                out=bank[:], lhsT=w2_codes[:, m].bitcast(FP8X4), lhsT_scale=w2_scales[:, m],
                rhs=x_by_hz[:].bitcast(FP8X4), rhs_scale=placed_scales[:, S : 2 * S], start=False, stop=True,
            )
            y.append(tile("y%d" % t, [P, S], F32))
            nc.scalar.copy(y[t][:], bank[:])
        for t in range(TILES):
            sg.append(tile("sg%d" % t, [P, S], F32))
            for a in range(0, S, HALF):
                nc.scalar.activation(
                    out=sg[t][:, a : a + HALF], in_=y[t][:].indirect(entries(n2_l, a, a + HALF)),
                    func=ACT.Sigmoid, scale=sl_rows[:, t : t + 1], bias=bias[:, t : t + 1],
                )

        def scatter(name, list_tile, src):
            window = tile(name, [P, WIDE], F32)
            nc.vector.tensor_copy(window[:].indirect(list_tile[:]), src[:])
            return window

        ds = [scatter("ds_%d" % t, n1_l, y[t]) for t in range(TILES)]

        pieces = d_picked[:].bitcast(I32).rearrange("p (a t w) -> p t a w", t=TILES, w=PIECE)
        early = tile("d_dealt_early", [P, VECTOR_DEALT, 2 * P], U32, "y0")
        nc.vector.tensor_copy(
            early[:].bitcast(I32).rearrange("p t (a w) -> p t a w", w=PIECE), pieces[:, 0:VECTOR_DEALT]
        )
        d_dealt = [early[:, t, :] for t in range(VECTOR_DEALT)]
        for t in range(VECTOR_DEALT, TILES):
            late = tile("d_dealt_late%d" % t, [P, 2 * P], U32)
            nc.sync.dma_start(late[:].bitcast(I32).rearrange("p (a w) -> p a w", w=PIECE), pieces[:, t])
            d_dealt.append(late[:])

        def make_z(name, a):
            rows = tile(name, [P, TILES, HALF], BF16, "z_rows")
            for t in range(TILES):
                nc.vector.scalar_tensor_tensor(
                    rows[:, t, :], ds[t][:, a : a + HALF], gs_rows[:, t : t + 1], sg[t][:, a : a + HALF],
                    ALU.mult, ALU.mult,
                )
            return rows[:].rearrange("p t c -> p c t")

        def second_product(bank_number, t, a, z_codes, z_scales):
            bank = open_bank(bank_number)
            for which in range(2):
                m = slice(which * P, (which + 1) * P)
                m_scales = slice((2 * t + which) * P, (2 * t + which + 1) * P)
                nc.tensor.matmul_mx(
                    out=bank[:, 0:HALF], lhsT=d_dealt[t][:, m].bitcast(FP8X4), lhsT_scale=d_dealt_scales[:, m_scales],
                    rhs=z_codes[:].bitcast(FP8X4), rhs_scale=z_scales[:], start=(which == 0), stop=(which == 1),
                )
            nc.scalar.activation(out=h2[t][:, a : a + HALF], in_=bank[:, 0:HALF], func=ACT.Copy, scale=0.0625)

        h2 = [tile("h2_%d" % t, [P, S], F32) for t in range(TILES)]

        z_first = tile("z_first", [P, HALF, PACK], BF16)
        nc.vector.tensor_copy(z_first[:], make_z("z_rows_first", 0))
        first_codes, first_scales = quantize("z_first", z_first[:].rearrange("p c t -> p (c t)"), HALF, "z_halves")
        for t in range(TILES):
            second_product(t, t, 0, first_codes, first_scales)
        z_rows_second = make_z("z_rows_second", HALF)
        z_second = tile("z_second", [P, HALF, PACK], BF16, "z_halves")
        nc.scalar.copy(z_second[:], z_rows_second)
        second_codes, second_scales = quantize("z_second", z_second[:].rearrange("p c t -> p (c t)"), HALF)
        ds2_after = ("", "", "z_rows", "z_halves")
        ds2 = [tile("ds2_%d" % t, [P, WIDE], F32, ds2_after[t]) for t in range(TILES)]
        for t in range(TILES):
            nc.vector.tensor_copy(ds2[t][:].indirect(entries(n3_l, 0, HALF)), h2[t][:, 0:HALF])
        for t in range(TILES):
            second_product(TILES + t, t, HALF, second_codes, second_scales)

        def add_turned(bank, term, first=False, last=False):
            for b in range(0, S, P):
                nc.tensor.matmul(
                    bank[:, b : b + P], term[:, b : b + P], identity[:],
                    start=(first and b == 0), stop=(last and b == S - P), is_transpose=True,
                )

        def through_scalar(name, src, func, scale):
            dst = tile(name, [P, S], F32)
            nc.scalar.activation(out=dst[:], in_=src[:], func=func, scale=scale)
            return dst

        def spare_bank(t):
            return open_bank(TILES + t % 2)

        h2_negated, h2_turned, st_bank = [], [], []
        for t in range(TILES):
            h2_negated.append(through_scalar("h2_negated%d" % t, h2[t], ACT.Copy, -1.0))
            bank = open_bank(t)
            add_turned(bank, h2[t], first=True, last=True)
            h2_turned.append(through_scalar("h2_turned%d" % t, bank, ACT.Copy, 1.0))
            st_bank.append(open_bank(t))
            add_turned(st_bank[t], h2_turned[t], first=True)

        out_rows = out.rearrange("(a t w) c -> t a w c", t=TILES, w=PIECE)
        st, out_bank = [], []
        for t in range(TILES):
            nc.vector.tensor_copy(ds2[t][:].indirect(entries(n3_l, HALF, S)), h2[t][:, HALF:S])
            bank = spare_bank(t)
            add_turned(bank, h2_negated[t], first=True)
            add_turned(bank, ds2[t], last=True)
            excess_turned = through_scalar("excess_turned%d" % t, bank, ACT.Relu, 1.0)
            add_turned(st_bank[t], excess_turned, last=True)
            st.append(through_scalar("st%d" % t, st_bank[t], ACT.Copy, 1.0))
            if t < TILES - 1:
                out_bank.append(open_bank(t))
                add_turned(out_bank[t], h2_turned[t], first=True)
                add_turned(out_bank[t], excess_turned)
        for t in range(TILES):
            ds3 = scatter("ds3_%d" % t, n4_l, st[t])
            if t < TILES - 1:
                bank = spare_bank(t)
                add_turned(bank, ds3, first=True, last=True)
                add_turned(out_bank[t], through_scalar("ds3_negated_turned%d" % t, bank, ACT.Copy, -1.0), last=True)
                result = through_scalar("result%d" % t, out_bank[t], ACT.Copy, 1.0)
                nc.scalar.dma_start(out_rows[t], result[:])
            else:
                result = tile("result%d" % t, [P, S], F32)
                for a in range(0, S, HALF):
                    half = slice(a, a + HALF)
                    nc.vector.tensor_tensor(result[:, half], st[t][:, half], ds3[:, half], ALU.subtract)
                    nc.sync.dma_start(out_rows[t][:, :, half], result[:, half])
